import numpy as np
import ml_dtypes


def mxq(x, axis, fmt="e4m3"):
    dtype, down = {"e4m3": (ml_dtypes.float8_e4m3fn, 7), "e5m2": (ml_dtypes.float8_e5m2, 14)}[fmt]
    v = np.moveaxis(np.asarray(x, np.float32).astype(ml_dtypes.bfloat16).astype(np.float64), axis, -1)
    blocks = v.reshape(v.shape[:-1] + (-1, 32))
    amax = np.abs(blocks).max(-1, keepdims=True)
    byte = np.maximum(np.where(amax > 0, np.frexp(amax)[1] - 1 + 127, 0) - down, 1)
    scale = np.exp2(byte - 127.0)
    codes = (blocks / scale).astype(np.float32).astype(dtype).astype(np.float64)
    return np.moveaxis((codes * scale).reshape(v.shape), -1, axis)


WIDE = False


def mx_kscale(k):
    if not WIDE:
        return np.ones(k)
    levels = np.array([10, -10, 5, -5, 0])
    if k % 512:
        return np.exp2(np.random.permutation(np.resize(levels, k // 32))).repeat(32)
    a = np.empty((k // 512, 16))
    for p in range(k // 512):
        a[p, :8] = np.random.permutation(np.resize(levels, 8))
        for g in range(8):
            far = levels[np.abs(levels - a[p, g]) >= 10]
            a[p, g + 8] = far[np.random.randint(len(far))]
    return np.exp2(a.ravel()).repeat(32)


def f64(x):
    return np.asarray(x).astype(np.float64)


def striped(idx):
    return np.tile(idx.reshape(-1, 16).T, (8, 1)).astype(np.uint16)


def unstriped(offs):
    return offs[:16].T.reshape(-1).astype(np.int64)


E2M1 = np.array([0.0, 0.5, 1.0, 1.5, 2.0, 3.0, 4.0, 6.0, -0.0, -0.5, -1.0, -1.5, -2.0, -3.0, -4.0, -6.0])


def pack_weight(w, fmt):
    k, n = w.shape
    w = f64(np.asarray(w, np.float32).astype(ml_dtypes.bfloat16)).reshape(k // 32, 32, n)
    amax = np.abs(w).max(1)
    if fmt == "e4m3":
        byte = np.frexp(amax)[1] - 1 + 127 - 7
    else:
        mant, ex = np.frexp(amax / 6.0)
        byte = np.where(mant > 0.5, ex, ex - 1) + 127
    byte = np.clip(np.where(amax > 0, byte, 1), 1, 254)
    scaled = (w * np.exp2(127.0 - byte)[:, None, :]).reshape(k, n).astype(np.float32)
    by_word = np.ascontiguousarray(scaled.reshape(k // 512, 128, 4, n).transpose(0, 1, 3, 2))
    if fmt == "e4m3":
        words = by_word.astype(ml_dtypes.float8_e4m3fn).view(np.uint8)
    else:
        c = by_word.astype(ml_dtypes.float4_e2m1fn).view(np.uint8) & 0xF
        words = (c[..., 0::2] | (c[..., 1::2] << 4)).reshape(k // 512, 128, 2 * n)
    return np.ascontiguousarray(words), np.ascontiguousarray(byte.astype(np.uint8).reshape(k // 512, 16, n))


def unpack_weight(words, scales, fmt):
    g, _, n = scales.shape
    words = np.ascontiguousarray(words).reshape(g, 128, n, -1)
    if fmt == "e4m3":
        vals = words.view(ml_dtypes.float8_e4m3fn).astype(np.float64)
    else:
        nib = np.empty((g, 128, n, 4), np.uint8)
        nib[..., 0::2] = words & 0xF
        nib[..., 1::2] = words >> 4
        vals = E2M1[nib]
    vals = vals * np.repeat(np.exp2(scales.astype(np.float64) - 127.0), 8, axis=1)[..., None]
    return vals.transpose(0, 1, 3, 2).reshape(g * 512, n)


def gelu(v):
    return 0.5 * v * (1.0 + np.tanh(np.sqrt(2.0 / np.pi) * (v + 0.044715 * v**3)))


K, K1, H, T, S, T3, S2, T2 = 1024, 512, 1024, 4096, 1024, 2048, 512, 2048


def setup_inputs():
    n = np.random.standard_normal
    s = mx_kscale(K)[:, None]
    u = s
    tab_words, tab_scales = pack_weight(n((K, T)) * s, "e4m3")
    tab2_words, tab2_scales = pack_weight(n((H, T3)) / np.sqrt(H) / u, "e4m3")
    w4_words, w4_scales = pack_weight(n((K - K1, H)) / np.sqrt(K) / s[K1:], "e2m1")
    return {
        "tab_words": tab_words, "tab_scales": tab_scales,
        "offs": striped(np.random.permutation(T)[:S]),
        "tab2_words": tab2_words, "tab2_scales": tab2_scales,
        "offs2": striped(np.random.permutation(T3)[:S2]),
        "offs3": striped(np.random.permutation(T2)[:S]),
        "w1": (n((K1, H)) / np.sqrt(K) / s[:K1]).astype(np.float32),
        "w4_words": w4_words, "w4_scales": w4_scales,
        "defence": (0.8 * n((H, S))).astype(np.float32),
        "gain": (1.2 * np.exp(0.3 * n(H)) * u[:, 0]).astype(np.float32),
        "keeper": (1.2 * np.exp(0.4 * n(S2))).astype(np.float32),
        "page1": n((S2, T2)).astype(np.float32),
        "wgo": np.exp(0.3 * n((128, S))).astype(np.float32),
    }


def reference(tab_words, tab_scales, offs, tab2_words, tab2_scales, offs2, offs3,
              w1, w4_words, w4_scales, defence, gain, keeper, page1, wgo):
    v = unpack_weight(tab_words, tab_scales, "e4m3")[:, unstriped(offs)]
    v2 = unpack_weight(tab2_words, tab2_scales, "e4m3")[:, unstriped(offs2)]
    w1q = mxq(f64(w1), 0, "e4m3")
    w4 = unpack_weight(w4_words, w4_scales, "e2m1")
    y = w1q.T @ v[:K1] + w4.T @ v[K1:]
    h = f64(gain)[:, None] * np.tanh(y + f64(defence))
    hq = mxq(h, 0, "e4m3")
    e = v2.T @ hq
    d = v2.T @ v
    best = np.maximum(f64(keeper)[:, None] * e, d)
    out = f64(page1).copy()
    out[:, unstriped(offs3)] = np.tile(f64(wgo), (S2 // 128, 1)) * best
    return out

@@ -1,0 +1,283 @@
+from contextlib import ExitStack
+
+import concourse.mybir as mybir
+
+F32 = mybir.dt.float32
+BF16 = mybir.dt.bfloat16
+I32 = mybir.dt.int32
+U32 = mybir.dt.uint32
+U16 = mybir.dt.uint16
+U8 = mybir.dt.uint8
+FP8X4 = mybir.dt.float8_e4m3fn_x4
+FP4X4 = mybir.dt.float4_e2m1fn_x4
+ACT = mybir.ActivationFunctionType
+ALU = mybir.AluOpType
+
+P = 128
+K, K1, H, T, S, T3, S2, T2 = 1024, 512, 1024, 4096, 1024, 2048, 512, 2048
+PACK = 4
+PASS = P * PACK
+BANK = 512
+HALF = S // 2
+CHUNKS = ((0, 256), (256, 256), (512, 512))
+NB = H // PASS
+NM = S2 // P
+
+FLOPS = 2 * K * H * S + 2 * 2 * H * S2 * S
+
+
+def tile_list_keeper_save_scores_kernel(
+    tc, tab_words, tab_scales, offs, tab2_words, tab2_scales, offs2, offs3,
+    w1, w4_words, w4_scales, defence, gain, keeper, page1, wgo, out,
+):
+    nc = tc.nc
+    with ExitStack() as ctx:
+        keep = ctx.enter_context(tc.tile_pool(name="keep", bufs=1))
+        work = ctx.enter_context(tc.tile_pool(name="work", bufs=2))
+        psum = ctx.enter_context(tc.psum_pool(name="psum", bufs=2))
+
+        def held(shape, dtype, name):
+            return keep.tile(shape, dtype, name=name, align_bytes=64)
+
+        idx1 = held([P, S // 16], U16, "idx1")
+        idx2 = held([P, S2 // 16], U16, "idx2")
+        idx3 = held([P, S // 16], U16, "idx3")
+        tabw = [held([P, T], U32, "tabw%d" % a) for a in range(2)]
+        tabs = held([P, 2, T], U8, "tabs")
+        tab2w = [held([P, T3], U32, "tab2w%d" % a) for a in range(2)]
+        tab2s = held([P, T3], U8, "tab2s")
+        w1raw = [held([P, PACK, PASS], F32, "w1raw%d" % b) for b in range(NB)]
+        w4raw = held([P, 2 * H], U8, "w4raw")
+        w4sraw = held([P, H], U8, "w4sraw")
+        w4w = held([P, 2 * H], U8, "w4w")
+        w4s = held([P, H], U8, "w4s")
+        w1w = [held([P, PASS], U32, "w1w%d" % b) for b in range(NB)]
+        w1s = [held([P, PASS], U8, "w1s%d" % b) for b in range(NB)]
+        gain_sb = held([P, NB, PACK], F32, "gain_sb")
+        keeper_sb = held([P, NM], F32, "keeper_sb")
+        wgo_sb = [held([P, S // 2], F32, "wgo%d" % i) for i in range(2)]
+        page = [held([P, T2], F32, "page%d" % m) for m in range(NM)]
+        vw = [held([P, S], U32, "vw%d" % a) for a in range(2)]
+        vs = [held([P, S], U8, "vs%d" % a) for a in range(2)]
+        v2w = [held([P, S2], U32, "v2w%d" % a) for a in range(2)]
+        v2s = held([P, S2], U8, "v2s")
+        v2_plane = (0, 4)
+
+        def load_words(dst, words, a):
+            nc.sync.dma_start(out=dst[:].bitcast(I32),
+                              in_=words[a].rearrange("p t i -> p (t i)").bitcast(I32))
+
+        dfc = {}
+
+        def load_defence(c, b):
+            c0, width = CHUNKS[c]
+            tag = "w1raw%d" % b if c == 2 else "dfc%d_%d" % (c, b)
+            dfc[(c, b)] = keep.tile([P, PACK, width], F32, name="dfc%d_%d" % (c, b), tag=tag,
+                                    align_bytes=64)
+            rows = defence[PASS * b: PASS * (b + 1), c0: c0 + width]
+            nc.sync.dma_start(out=dfc[(c, b)][:], in_=rows.rearrange("(p t) n -> p t n", t=PACK))
+
+        def load_w1(b):
+            nc.sync.dma_start(
+                out=w1raw[b][:],
+                in_=w1[:, PASS * b: PASS * (b + 1)].rearrange("(p j) r -> p j r", j=PACK))
+
+        def load_page(m):
+            nc.sync.dma_start(out=page[m][:], in_=page1[P * m: P * (m + 1), :])
+
+        def load_wgo(i):
+            nc.sync.dma_start(out=wgo_sb[i][:], in_=wgo[:, S // 2 * i: S // 2 * (i + 1)])
+
+        nc.vector.memset(tabs[:, 0, :].bitcast(I32), 0)
+        nc.gpsimd.memset(tabs[:, 1, :].bitcast(I32), 0)
+        nc.vector.memset(w4sraw[:].bitcast(I32), 0)
+        nc.vector.memset(tab2s[:].bitcast(I32), 0)
+        nc.sync.dma_start(idx1[:], offs)
+        nc.sync.dma_start(out=w4raw[:].bitcast(I32), in_=w4_words[0].bitcast(I32))
+        for q in range(4):
+            nc.sync.dma_start(
+                out=tabs[32 * q: 32 * q + 4, :, :].bitcast(I32),
+                in_=tab_scales[:, 4 * q: 4 * q + 4, :].rearrange("a r t -> r a t").bitcast(I32))
+        load_words(tabw[0], tab_words, 0)
+        load_w1(0)
+        for q in range(4):
+            nc.sync.dma_start(
+                out=w4sraw[32 * q: 32 * q + 4, :].bitcast(I32),
+                in_=w4_scales[0, 4 * q: 4 * q + 4, :].bitcast(I32))
+        nc.sync.dma_start(idx2[:], offs2)
+        load_w1(1)
+        load_words(tabw[1], tab_words, 1)
+        for q in range(4):
+            nc.sync.dma_start(
+                out=tab2s[32 * q: 32 * q + 8, :].bitcast(I32),
+                in_=tab2_scales[:, 4 * q: 4 * q + 4, :].bitcast(I32))
+        nc.sync.dma_start(out=gain_sb[:], in_=gain.rearrange("(b p t) -> p b t", b=NB, t=PACK))
+
+        nc.vector.tensor_copy(
+            out=w4w[:].bitcast(U16).rearrange("p (b t m) -> p b t m", b=NB, t=PACK),
+            in_=w4raw[:].bitcast(U16).rearrange("p (b m t) -> p b t m", b=NB, t=PACK))
+        for a in range(2):
+            nc.vector.tensor_copy(vs[a][:], tabs[:, a, :].indirect(idx1[:]))
+        nc.vector.tensor_copy(vw[0][:], tabw[0][:].indirect(idx1[:]))
+
+        def quantize_w1(b):
+            w1b = work.tile([P, PASS * PACK], BF16, name="w1b", align_bytes=64)
+            nc.scalar.copy(
+                out=w1b[:].rearrange("p (t g i j) -> p g j i t", t=PACK, i=2, j=PACK),
+                in_=w1raw[b][:].rearrange("p j (g i t) -> p g j i t", i=2, t=PACK))
+            nc.vector.quantize_mx(out=w1w[b][:].bitcast(FP8X4), scales=w1s[b][:], in_=w1b[:])
+
+        quantize_w1(0)
+        nc.vector.tensor_copy(
+            out=w4s[:].rearrange("p (b t m) -> p b t m", b=NB, t=PACK),
+            in_=w4sraw[:].rearrange("p (b m t) -> p b t m", b=NB, t=PACK))
+        quantize_w1(1)
+
+        load_defence(0, 0)
+        load_defence(0, 1)
+        load_defence(1, 0)
+        load_defence(1, 1)
+        load_words(tab2w[0], tab2_words, 0)
+        nc.sync.dma_start(out=keeper_sb[:], in_=keeper.rearrange("(m p) -> p m", p=P),
+                          allow_slow_non_contiguous=True)
+        nc.sync.dma_start(idx3[:], offs3)
+        load_words(tab2w[1], tab2_words, 1)
+        load_defence(2, 0)
+        load_wgo(0)
+        load_page(0)
+        load_defence(2, 1)
+        load_page(1)
+        load_page(2)
+        load_wgo(1)
+        load_page(3)
+
+        def gather_v1(c):
+            c0, width = CHUNKS[c]
+            nc.vector.tensor_copy(
+                vw[1][:, c0: c0 + width], tabw[1][:].indirect(idx1[:, c0 // 16: (c0 + width) // 16]))
+
+        zs = {}
+
+        def throw_sums(c, b):
+            c0, width = CHUNKS[c]
+            cols = slice(c0, c0 + width)
+            per_bank = BANK // width
+            z = work.tile([P, PACK, width], F32, name="z", bufs=3)
+            for t0 in range(0, PACK, per_bank):
+                y = psum.tile([P, per_bank, width], F32, name="y", bufs=4)
+                for u in range(per_bank):
+                    t = t0 + u
+                    wc = slice(P * t, P * (t + 1))
+                    r0 = PASS * b + P * t
+                    nc.tensor.matmul_mx(
+                        out=y[:, u, :], lhsT=w1w[b][:, wc].bitcast(FP8X4), lhsT_scale=w1s[b][:, wc],
+                        rhs=vw[0][:, cols].bitcast(FP8X4), rhs_scale=vs[0][:, cols],
+                        start=True, stop=False)
+                    nc.tensor.matmul_mx(
+                        out=y[:, u, :], lhsT=w4w[:, 2 * r0: 2 * (r0 + P)].bitcast(FP4X4),
+                        lhsT_scale=w4s[:, r0: r0 + P],
+                        rhs=vw[1][:, cols].bitcast(FP8X4), rhs_scale=vs[1][:, cols],
+                        start=False, stop=True)
+                nc.vector.tensor_tensor(z[:, t0: t0 + per_bank, :], y[:],
+                                        dfc[(c, b)][:, t0: t0 + per_bank, :], ALU.add)
+            zs[(c, b)] = z
+
+        hin = [held([P, NB, width * PACK], BF16, "hin%d" % c) for c, (c0, width) in enumerate(CHUNKS)]
+        hw = [held([P, NB * width], U32, "hw%d" % c) for c, (c0, width) in enumerate(CHUNKS)]
+        hs = [held([P, NB * width], U8, "hs%d" % c) for c, (c0, width) in enumerate(CHUNKS)]
+
+        def make_h(c, b):
+            width = CHUNKS[c][1]
+            z = zs[(c, b)]
+            if c == 0:
+                th = work.tile([P, PACK * width], F32, name="th")
+                nc.scalar.activation(
+                    out=th[:].rearrange("p (g i t) -> p g t i", i=4, t=PACK),
+                    in_=z[:].rearrange("p t (g i) -> p g t i", i=4), func=ACT.Tanh)
+                nc.vector.tensor_tensor(
+                    hin[c][:, b, :].rearrange("p (n t) -> p n t", t=PACK),
+                    th[:].rearrange("p (n t) -> p n t", t=PACK),
+                    gain_sb[:, b, :].rearrange("p (o t) -> p o t", o=1).to_broadcast([P, width, PACK]),
+                    ALU.mult)
+            else:
+                flat = z[:].rearrange("p t n -> p (t n)")
+                nc.scalar.activation(out=flat, in_=flat, func=ACT.Tanh)
+                hb = work.tile([P, PACK, width], BF16, name="hb", tag="w1b", align_bytes=64)
+                for t in range(PACK):
+                    nc.scalar.activation(out=hb[:, t, :], in_=z[:, t, :],
+                                         func=ACT.Copy, scale=gain_sb[:, b, t: t + 1])
+                nc.scalar.copy(
+                    out=hin[c][:, b, :].rearrange("p (g i t) -> p g t i", i=8, t=PACK),
+                    in_=hb[:].rearrange("p t (g i) -> p g t i", i=8))
+
+        def quantize_h(c):
+            nc.vector.quantize_mx(out=hw[c][:].bitcast(FP8X4), scales=hs[c][:],
+                                  in_=hin[c][:].rearrange("p b n -> p (b n)"))
+
+        direct = {}
+
+        def direct_scores(half, m):
+            cols = slice(HALF * half, HALF * (half + 1))
+            mc = slice(P * m, P * (m + 1))
+            d = psum.tile([P, HALF], F32, name="d")
+            for a in range(2):
+                nc.tensor.matmul_mx(
+                    out=d[:], lhsT=v2w[a][:, mc].bitcast(FP8X4), lhsT_scale=v2s[v2_plane[a]:P, mc],
+                    rhs=vw[a][:, cols].bitcast(FP8X4), rhs_scale=vs[a][:, cols],
+                    start=(a == 0), stop=(a == 1))
+            dsb = work.tile([P, HALF], F32, name="dsb", bufs=4)
+            nc.scalar.copy(out=dsb[:], in_=d[:])
+            direct[(half, m)] = dsb
+
+        def place(half, m):
+            mc = slice(P * m, P * (m + 1))
+            e = psum.tile([P, HALF], F32, name="e")
+            for c, (c0, width) in enumerate(CHUNKS):
+                if c0 // HALF != half:
+                    continue
+                for a in range(2):
+                    hc = slice(width * a, width * (a + 1))
+                    nc.tensor.matmul_mx(
+                        out=e[:, c0 % HALF: c0 % HALF + width],
+                        lhsT=v2w[a][:, mc].bitcast(FP8X4), lhsT_scale=v2s[v2_plane[a]:P, mc],
+                        rhs=hw[c][:, hc].bitcast(FP8X4), rhs_scale=hs[c][:, hc],
+                        start=(a == 0), stop=(a == 1))
+            bst = work.tile([P, HALF], F32, name="bst", bufs=2)
+            nc.vector.scalar_tensor_tensor(bst[:], e[:], keeper_sb[:, m: m + 1],
+                                           direct[(half, m)][:], ALU.mult, ALU.max)
+            nc.vector.tensor_tensor(
+                page[m][:].indirect(idx3[:, HALF * half // 16: HALF * (half + 1) // 16]),
+                bst[:], wgo_sb[half][:], ALU.mult)
+            if half == 1:
+                nc.sync.dma_start(out=out[P * m: P * (m + 1), :], in_=page[m][:])
+
+        nc.vector.tensor_copy(v2s[:], tab2s[:].indirect(idx2[:]))
+        gather_v1(0)
+        gather_v1(1)
+        throw_sums(0, 0)
+        gather_v1(2)
+        throw_sums(0, 1)
+        make_h(0, 0)
+        throw_sums(1, 0)
+        make_h(0, 1)
+        throw_sums(1, 1)
+        quantize_h(0)
+        nc.vector.tensor_copy(v2w[0][:], tab2w[0][:].indirect(idx2[:]))
+        nc.vector.tensor_copy(v2w[1][:], tab2w[1][:].indirect(idx2[:]))
+        make_h(1, 0)
+        make_h(1, 1)
+        throw_sums(2, 0)
+        quantize_h(1)
+        for m in range(NM):
+            direct_scores(0, m)
+        make_h(2, 0)
+        place(0, 0)
+        throw_sums(2, 1)
+        make_h(2, 1)
+        for m in range(1, NM):
+            place(0, m)
+        for m in range(NM):
+            direct_scores(1, m)
+        quantize_h(2)
+        for m in range(NM):
+            place(1, m)

@@ -17,11 +17,11 @@ P = 128
 K, K1, H, T, S, T3, S2, T2 = 1024, 512, 1024, 4096, 1024, 2048, 512, 2048
 PACK = 4
 PASS = P * PACK
-BANK = 512
 HALF = S // 2
-CHUNKS = ((0, 256), (256, 256), (512, 512))
 NB = H // PASS
 NM = S2 // P
+V_PLANE = (4, 0)
+V2_PLANE = (8, 12)
 
 FLOPS = 2 * K * H * S + 2 * 2 * H * S2 * S
 
@@ -43,7 +43,7 @@ def tile_list_keeper_save_scores_kernel(
         idx2 = held([P, S2 // 16], U16, "idx2")
         idx3 = held([P, S // 16], U16, "idx3")
         tabw = [held([P, T], U32, "tabw%d" % a) for a in range(2)]
-        tabs = held([P, 2, T], U8, "tabs")
+        tabs = held([P, T], U8, "tabs")
         tab2w = [held([P, T3], U32, "tab2w%d" % a) for a in range(2)]
         tab2s = held([P, T3], U8, "tab2s")
         w1raw = [held([P, PACK, PASS], F32, "w1raw%d" % b) for b in range(NB)]
@@ -55,27 +55,36 @@ def tile_list_keeper_save_scores_kernel(
         w1s = [held([P, PASS], U8, "w1s%d" % b) for b in range(NB)]
         gain_sb = held([P, NB, PACK], F32, "gain_sb")
         keeper_sb = held([P, NM], F32, "keeper_sb")
-        wgo_sb = [held([P, S // 2], F32, "wgo%d" % i) for i in range(2)]
+        wgo_sb = [held([P, HALF], F32, "wgo%d" % i) for i in range(2)]
         page = [held([P, T2], F32, "page%d" % m) for m in range(NM)]
         vw = [held([P, S], U32, "vw%d" % a) for a in range(2)]
-        vs = [held([P, S], U8, "vs%d" % a) for a in range(2)]
+        vs = held([P, S], U8, "vs")
         v2w = [held([P, S2], U32, "v2w%d" % a) for a in range(2)]
         v2s = held([P, S2], U8, "v2s")
-        v2_plane = (0, 4)
+        hin = {(half, b): held([P, HALF * PACK], BF16, "hin%d_%d" % (half, b))
+               for half in range(2) for b in range(NB)}
+        hw = {(half, b): held([P, HALF], U32, "hw%d_%d" % (half, b))
+              for half in range(2) for b in range(NB)}
+        hs = {(half, b): held([P, HALF], U8, "hs%d_%d" % (half, b))
+              for half in range(2) for b in range(NB)}
 
         def load_words(dst, words, a):
             nc.sync.dma_start(out=dst[:].bitcast(I32),
                               in_=words[a].rearrange("p t i -> p (t i)").bitcast(I32))
 
+        def load_plane(dst, scales, a, row0):
+            for q in range(4):
+                nc.sync.dma_start(
+                    out=dst[32 * q + row0: 32 * q + row0 + 4, :].bitcast(I32),
+                    in_=scales[a, 4 * q: 4 * q + 4, :].bitcast(I32))
+
         dfc = {}
 
-        def load_defence(c, b):
-            c0, width = CHUNKS[c]
-            tag = "w1raw%d" % b if c == 2 else "dfc%d_%d" % (c, b)
-            dfc[(c, b)] = keep.tile([P, PACK, width], F32, name="dfc%d_%d" % (c, b), tag=tag,
-                                    align_bytes=64)
-            rows = defence[PASS * b: PASS * (b + 1), c0: c0 + width]
-            nc.sync.dma_start(out=dfc[(c, b)][:], in_=rows.rearrange("(p t) n -> p t n", t=PACK))
+        def load_defence(half, b):
+            tag = "w1raw%d" % b if half == 1 else "dfc%d" % b
+            dfc[(half, b)] = keep.tile([P, PACK, HALF], F32, name="dfc", tag=tag, align_bytes=64)
+            rows = defence[PASS * b: PASS * (b + 1), HALF * half: HALF * (half + 1)]
+            nc.sync.dma_start(out=dfc[(half, b)][:], in_=rows.rearrange("(p t) n -> p t n", t=PACK))
 
         def load_w1(b):
             nc.sync.dma_start(
@@ -86,39 +95,7 @@ def tile_list_keeper_save_scores_kernel(
             nc.sync.dma_start(out=page[m][:], in_=page1[P * m: P * (m + 1), :])
 
         def load_wgo(i):
-            nc.sync.dma_start(out=wgo_sb[i][:], in_=wgo[:, S // 2 * i: S // 2 * (i + 1)])
-
-        nc.vector.memset(tabs[:, 0, :].bitcast(I32), 0)
-        nc.gpsimd.memset(tabs[:, 1, :].bitcast(I32), 0)
-        nc.vector.memset(w4sraw[:].bitcast(I32), 0)
-        nc.vector.memset(tab2s[:].bitcast(I32), 0)
-        nc.sync.dma_start(idx1[:], offs)
-        nc.sync.dma_start(out=w4raw[:].bitcast(I32), in_=w4_words[0].bitcast(I32))
-        for q in range(4):
-            nc.sync.dma_start(
-                out=tabs[32 * q: 32 * q + 4, :, :].bitcast(I32),
-                in_=tab_scales[:, 4 * q: 4 * q + 4, :].rearrange("a r t -> r a t").bitcast(I32))
-        load_words(tabw[0], tab_words, 0)
-        load_w1(0)
-        for q in range(4):
-            nc.sync.dma_start(
-                out=w4sraw[32 * q: 32 * q + 4, :].bitcast(I32),
-                in_=w4_scales[0, 4 * q: 4 * q + 4, :].bitcast(I32))
-        nc.sync.dma_start(idx2[:], offs2)
-        load_w1(1)
-        load_words(tabw[1], tab_words, 1)
-        for q in range(4):
-            nc.sync.dma_start(
-                out=tab2s[32 * q: 32 * q + 8, :].bitcast(I32),
-                in_=tab2_scales[:, 4 * q: 4 * q + 4, :].bitcast(I32))
-        nc.sync.dma_start(out=gain_sb[:], in_=gain.rearrange("(b p t) -> p b t", b=NB, t=PACK))
-
-        nc.vector.tensor_copy(
-            out=w4w[:].bitcast(U16).rearrange("p (b t m) -> p b t m", b=NB, t=PACK),
-            in_=w4raw[:].bitcast(U16).rearrange("p (b m t) -> p b t m", b=NB, t=PACK))
-        for a in range(2):
-            nc.vector.tensor_copy(vs[a][:], tabs[:, a, :].indirect(idx1[:]))
-        nc.vector.tensor_copy(vw[0][:], tabw[0][:].indirect(idx1[:]))
+            nc.sync.dma_start(out=wgo_sb[i][:], in_=wgo[:, HALF * i: HALF * (i + 1)])
 
         def quantize_w1(b):
             w1b = work.tile([P, PASS * PACK], BF16, name="w1b", align_bytes=64)
@@ -127,7 +104,123 @@ def tile_list_keeper_save_scores_kernel(
                 in_=w1raw[b][:].rearrange("p j (g i t) -> p g j i t", i=2, t=PACK))
             nc.vector.quantize_mx(out=w1w[b][:].bitcast(FP8X4), scales=w1s[b][:], in_=w1b[:])
 
+        def list_half(idx, half):
+            return idx[:, HALF * half // 16: HALF * (half + 1) // 16]
+
+        def gather_v1(half):
+            nc.vector.tensor_copy(vw[1][:, HALF * half: HALF * (half + 1)],
+                                  tabw[1][:].indirect(list_half(idx1, half)))
+
+        zs = {}
+
+        def throw_sums(half, b):
+            cols = slice(HALF * half, HALF * (half + 1))
+            z = work.tile([P, PACK, HALF], F32, name="z", bufs=3)
+            for t in range(PACK):
+                y = psum.tile([P, HALF], F32, name="y", bufs=4)
+                wc = slice(P * t, P * (t + 1))
+                r0 = PASS * b + P * t
+                nc.tensor.matmul_mx(
+                    out=y[:], lhsT=w1w[b][:, wc].bitcast(FP8X4), lhsT_scale=w1s[b][:, wc],
+                    rhs=vw[0][:, cols].bitcast(FP8X4), rhs_scale=vs[V_PLANE[0]:P, cols],
+                    start=True, stop=False)
+                nc.tensor.matmul_mx(
+                    out=y[:], lhsT=w4w[:, 2 * r0: 2 * (r0 + P)].bitcast(FP4X4),
+                    lhsT_scale=w4s[:, r0: r0 + P],
+                    rhs=vw[1][:, cols].bitcast(FP8X4), rhs_scale=vs[V_PLANE[1]:P, cols],
+                    start=False, stop=True)
+                nc.vector.tensor_tensor(z[:, t, :], y[:], dfc[(half, b)][:, t, :], ALU.add)
+            zs[(half, b)] = z
+
+        def make_h(half, b):
+            z = zs[(half, b)]
+            if (half, b) == (0, 0):
+                th = held([P, PACK * HALF], F32, "th")
+                nc.scalar.activation(
+                    out=th[:].rearrange("p (g i t) -> p g t i", i=4, t=PACK),
+                    in_=z[:].rearrange("p t (g i) -> p g t i", i=4), func=ACT.Tanh)
+                nc.vector.tensor_tensor(
+                    hin[(half, b)][:].rearrange("p (n t) -> p n t", t=PACK),
+                    th[:].rearrange("p (n t) -> p n t", t=PACK),
+                    gain_sb[:, b, :].rearrange("p (o t) -> p o t", o=1).to_broadcast([P, HALF, PACK]),
+                    ALU.mult)
+            else:
+                flat = z[:].rearrange("p t n -> p (t n)")
+                nc.scalar.activation(out=flat, in_=flat, func=ACT.Tanh)
+                hb = work.tile([P, PACK, HALF], BF16, name="hb", tag="w1b", align_bytes=64)
+                for t in range(PACK):
+                    nc.scalar.activation(out=hb[:, t, :], in_=z[:, t, :],
+                                         func=ACT.Copy, scale=gain_sb[:, b, t: t + 1])
+                nc.scalar.copy(
+                    out=hin[(half, b)][:].rearrange("p (g i t) -> p g t i", i=8, t=PACK),
+                    in_=hb[:].rearrange("p t (g i) -> p g t i", i=8))
+
+        def quantize_h(half, b):
+            nc.vector.quantize_mx(out=hw[(half, b)][:].bitcast(FP8X4), scales=hs[(half, b)][:],
+                                  in_=hin[(half, b)][:])
+
+        def profile_sum(name, m, words, scales):
+            mc = slice(P * m, P * (m + 1))
+            acc = psum.tile([P, HALF], F32, name=name)
+            for a in range(2):
+                nc.tensor.matmul_mx(
+                    out=acc[:], lhsT=v2w[a][:, mc].bitcast(FP8X4), lhsT_scale=v2s[V2_PLANE[a]:P, mc],
+                    rhs=words[a].bitcast(FP8X4), rhs_scale=scales[a], start=(a == 0), stop=(a == 1))
+            return acc
+
+        direct = {}
+
+        def direct_scores(half, m):
+            cols = slice(HALF * half, HALF * (half + 1))
+            d = profile_sum("d", m, [vw[a][:, cols] for a in range(2)],
+                            [vs[V_PLANE[a]:P, cols] for a in range(2)])
+            dsb = work.tile([P, HALF], F32, name="dsb", bufs=2)
+            nc.scalar.copy(out=dsb[:], in_=d[:])
+            direct[(half, m)] = dsb
+
+        best = {}
+
+        def best_scores(half, m):
+            e = profile_sum("e", m, [hw[(half, b)][:] for b in range(NB)],
+                            [hs[(half, b)][:] for b in range(NB)])
+            bst = work.tile([P, HALF], F32, name="bst", bufs=3)
+            nc.vector.scalar_tensor_tensor(bst[:], e[:], keeper_sb[:, m: m + 1],
+                                           direct[(half, m)][:], ALU.mult, ALU.max)
+            best[(half, m)] = bst
+
+        def place(half, m):
+            nc.vector.tensor_tensor(page[m][:].indirect(list_half(idx3, half)),
+                                    best[(half, m)][:], wgo_sb[half][:], ALU.mult)
+            if half == 1:
+                nc.sync.dma_start(out=out[P * m: P * (m + 1), :], in_=page[m][:])
+
+        nc.vector.memset(tabs[:].bitcast(I32), 0)
+        nc.gpsimd.memset(w4sraw[:].bitcast(I32), 0)
+        nc.gpsimd.memset(tab2s[:].bitcast(I32), 0)
+        nc.sync.dma_start(idx1[:], offs)
+        nc.sync.dma_start(out=w4raw[:].bitcast(I32), in_=w4_words[0].bitcast(I32))
+        load_plane(tabs, tab_scales, 0, V_PLANE[0])
+        load_words(tabw[0], tab_words, 0)
+        load_w1(0)
+        load_plane(tabs, tab_scales, 1, V_PLANE[1])
+        nc.sync.dma_start(idx2[:], offs2)
+        nc.sync.dma_start(out=gain_sb[:], in_=gain.rearrange("(b p t) -> p b t", b=NB, t=PACK))
+        load_words(tabw[1], tab_words, 1)
+        load_plane(w4sraw, w4_scales, 0, 0)
+        load_w1(1)
+        for q in range(4):
+            nc.sync.dma_start(
+                out=tab2s[32 * q + V2_PLANE[0]: 32 * q + V2_PLANE[0] + 8, :].bitcast(I32),
+                in_=tab2_scales[:, 4 * q: 4 * q + 4, :].bitcast(I32))
+
+        nc.vector.tensor_copy(
+            out=w4w[:].bitcast(U16).rearrange("p (b t m) -> p b t m", b=NB, t=PACK),
+            in_=w4raw[:].bitcast(U16).rearrange("p (b m t) -> p b t m", b=NB, t=PACK))
+        nc.vector.tensor_copy(vw[0][:], tabw[0][:].indirect(idx1[:]))
+        nc.vector.tensor_copy(vs[:], tabs[:].indirect(idx1[:]))
         quantize_w1(0)
+        gather_v1(0)
+        gather_v1(1)
         nc.vector.tensor_copy(
             out=w4s[:].rearrange("p (b t m) -> p b t m", b=NB, t=PACK),
             in_=w4sraw[:].rearrange("p (b m t) -> p b t m", b=NB, t=PACK))
@@ -135,149 +228,49 @@ def tile_list_keeper_save_scores_kernel(
 
         load_defence(0, 0)
         load_defence(0, 1)
-        load_defence(1, 0)
-        load_defence(1, 1)
         load_words(tab2w[0], tab2_words, 0)
         nc.sync.dma_start(out=keeper_sb[:], in_=keeper.rearrange("(m p) -> p m", p=P),
                           allow_slow_non_contiguous=True)
         nc.sync.dma_start(idx3[:], offs3)
         load_words(tab2w[1], tab2_words, 1)
-        load_defence(2, 0)
+        load_defence(1, 0)
         load_wgo(0)
         load_page(0)
-        load_defence(2, 1)
+        load_defence(1, 1)
         load_page(1)
         load_page(2)
         load_wgo(1)
         load_page(3)
 
-        def gather_v1(c):
-            c0, width = CHUNKS[c]
-            nc.vector.tensor_copy(
-                vw[1][:, c0: c0 + width], tabw[1][:].indirect(idx1[:, c0 // 16: (c0 + width) // 16]))
-
-        zs = {}
-
-        def throw_sums(c, b):
-            c0, width = CHUNKS[c]
-            cols = slice(c0, c0 + width)
-            per_bank = BANK // width
-            z = work.tile([P, PACK, width], F32, name="z", bufs=3)
-            for t0 in range(0, PACK, per_bank):
-                y = psum.tile([P, per_bank, width], F32, name="y", bufs=4)
-                for u in range(per_bank):
-                    t = t0 + u
-                    wc = slice(P * t, P * (t + 1))
-                    r0 = PASS * b + P * t
-                    nc.tensor.matmul_mx(
-                        out=y[:, u, :], lhsT=w1w[b][:, wc].bitcast(FP8X4), lhsT_scale=w1s[b][:, wc],
-                        rhs=vw[0][:, cols].bitcast(FP8X4), rhs_scale=vs[0][:, cols],
-                        start=True, stop=False)
-                    nc.tensor.matmul_mx(
-                        out=y[:, u, :], lhsT=w4w[:, 2 * r0: 2 * (r0 + P)].bitcast(FP4X4),
-                        lhsT_scale=w4s[:, r0: r0 + P],
-                        rhs=vw[1][:, cols].bitcast(FP8X4), rhs_scale=vs[1][:, cols],
-                        start=False, stop=True)
-                nc.vector.tensor_tensor(z[:, t0: t0 + per_bank, :], y[:],
-                                        dfc[(c, b)][:, t0: t0 + per_bank, :], ALU.add)
-            zs[(c, b)] = z
-
-        hin = [held([P, NB, width * PACK], BF16, "hin%d" % c) for c, (c0, width) in enumerate(CHUNKS)]
-        hw = [held([P, NB * width], U32, "hw%d" % c) for c, (c0, width) in enumerate(CHUNKS)]
-        hs = [held([P, NB * width], U8, "hs%d" % c) for c, (c0, width) in enumerate(CHUNKS)]
-
-        def make_h(c, b):
-            width = CHUNKS[c][1]
-            z = zs[(c, b)]
-            if c == 0:
-                th = work.tile([P, PACK * width], F32, name="th")
-                nc.scalar.activation(
-                    out=th[:].rearrange("p (g i t) -> p g t i", i=4, t=PACK),
-                    in_=z[:].rearrange("p t (g i) -> p g t i", i=4), func=ACT.Tanh)
-                nc.vector.tensor_tensor(
-                    hin[c][:, b, :].rearrange("p (n t) -> p n t", t=PACK),
-                    th[:].rearrange("p (n t) -> p n t", t=PACK),
-                    gain_sb[:, b, :].rearrange("p (o t) -> p o t", o=1).to_broadcast([P, width, PACK]),
-                    ALU.mult)
-            else:
-                flat = z[:].rearrange("p t n -> p (t n)")
-                nc.scalar.activation(out=flat, in_=flat, func=ACT.Tanh)
-                hb = work.tile([P, PACK, width], BF16, name="hb", tag="w1b", align_bytes=64)
-                for t in range(PACK):
-                    nc.scalar.activation(out=hb[:, t, :], in_=z[:, t, :],
-                                         func=ACT.Copy, scale=gain_sb[:, b, t: t + 1])
-                nc.scalar.copy(
-                    out=hin[c][:, b, :].rearrange("p (g i t) -> p g t i", i=8, t=PACK),
-                    in_=hb[:].rearrange("p t (g i) -> p g t i", i=8))
-
-        def quantize_h(c):
-            nc.vector.quantize_mx(out=hw[c][:].bitcast(FP8X4), scales=hs[c][:],
-                                  in_=hin[c][:].rearrange("p b n -> p (b n)"))
-
-        direct = {}
-
-        def direct_scores(half, m):
-            cols = slice(HALF * half, HALF * (half + 1))
-            mc = slice(P * m, P * (m + 1))
-            d = psum.tile([P, HALF], F32, name="d")
-            for a in range(2):
-                nc.tensor.matmul_mx(
-                    out=d[:], lhsT=v2w[a][:, mc].bitcast(FP8X4), lhsT_scale=v2s[v2_plane[a]:P, mc],
-                    rhs=vw[a][:, cols].bitcast(FP8X4), rhs_scale=vs[a][:, cols],
-                    start=(a == 0), stop=(a == 1))
-            dsb = work.tile([P, HALF], F32, name="dsb", bufs=4)
-            nc.scalar.copy(out=dsb[:], in_=d[:])
-            direct[(half, m)] = dsb
-
-        def place(half, m):
-            mc = slice(P * m, P * (m + 1))
-            e = psum.tile([P, HALF], F32, name="e")
-            for c, (c0, width) in enumerate(CHUNKS):
-                if c0 // HALF != half:
-                    continue
-                for a in range(2):
-                    hc = slice(width * a, width * (a + 1))
-                    nc.tensor.matmul_mx(
-                        out=e[:, c0 % HALF: c0 % HALF + width],
-                        lhsT=v2w[a][:, mc].bitcast(FP8X4), lhsT_scale=v2s[v2_plane[a]:P, mc],
-                        rhs=hw[c][:, hc].bitcast(FP8X4), rhs_scale=hs[c][:, hc],
-                        start=(a == 0), stop=(a == 1))
-            bst = work.tile([P, HALF], F32, name="bst", bufs=2)
-            nc.vector.scalar_tensor_tensor(bst[:], e[:], keeper_sb[:, m: m + 1],
-                                           direct[(half, m)][:], ALU.mult, ALU.max)
-            nc.vector.tensor_tensor(
-                page[m][:].indirect(idx3[:, HALF * half // 16: HALF * (half + 1) // 16]),
-                bst[:], wgo_sb[half][:], ALU.mult)
-            if half == 1:
-                nc.sync.dma_start(out=out[P * m: P * (m + 1), :], in_=page[m][:])
-
         nc.vector.tensor_copy(v2s[:], tab2s[:].indirect(idx2[:]))
-        gather_v1(0)
-        gather_v1(1)
         throw_sums(0, 0)
-        gather_v1(2)
         throw_sums(0, 1)
         make_h(0, 0)
-        throw_sums(1, 0)
         make_h(0, 1)
-        throw_sums(1, 1)
-        quantize_h(0)
-        nc.vector.tensor_copy(v2w[0][:], tab2w[0][:].indirect(idx2[:]))
-        nc.vector.tensor_copy(v2w[1][:], tab2w[1][:].indirect(idx2[:]))
-        make_h(1, 0)
-        make_h(1, 1)
-        throw_sums(2, 0)
-        quantize_h(1)
+        for a in range(2):
+            nc.vector.tensor_copy(v2w[a][:], tab2w[a][:].indirect(idx2[:]))
+        quantize_h(0, 0)
+        throw_sums(1, 0)
+        quantize_h(0, 1)
         for m in range(NM):
             direct_scores(0, m)
-        make_h(2, 0)
+        make_h(1, 0)
+        best_scores(0, 0)
+        best_scores(0, 1)
         place(0, 0)
-        throw_sums(2, 1)
-        make_h(2, 1)
-        for m in range(1, NM):
-            place(0, m)
+        throw_sums(1, 1)
+        make_h(1, 1)
+        best_scores(0, 2)
+        place(0, 1)
+        best_scores(0, 3)
+        place(0, 2)
+        quantize_h(1, 0)
+        place(0, 3)
         for m in range(NM):
             direct_scores(1, m)
-        quantize_h(2)
+        quantize_h(1, 1)
+        best_scores(1, 0)
         for m in range(NM):
+            if m + 1 < NM:
+                best_scores(1, m + 1)
             place(1, m)

@@ -33,8 +33,7 @@ def tile_list_keeper_save_scores_kernel(
     nc = tc.nc
     with ExitStack() as ctx:
         keep = ctx.enter_context(tc.tile_pool(name="keep", bufs=1))
-        work = ctx.enter_context(tc.tile_pool(name="work", bufs=2))
-        psum = ctx.enter_context(tc.psum_pool(name="psum", bufs=2))
+        psum = ctx.enter_context(tc.psum_pool(name="psum", bufs=1))
 
         def held(shape, dtype, name):
             return keep.tile(shape, dtype, name=name, align_bytes=64)
@@ -57,34 +56,40 @@ def tile_list_keeper_save_scores_kernel(
         keeper_sb = held([P, NM], F32, "keeper_sb")
         wgo_sb = [held([P, HALF], F32, "wgo%d" % i) for i in range(2)]
         page = [held([P, T2], F32, "page%d" % m) for m in range(NM)]
-        vw = [held([P, S], U32, "vw%d" % a) for a in range(2)]
+        vw0 = held([P, S], U32, "vw0")
+        vw1 = {}
         vs = held([P, S], U8, "vs")
         v2w = [held([P, S2], U32, "v2w%d" % a) for a in range(2)]
         v2s = held([P, S2], U8, "v2s")
-        hin = {(half, b): held([P, HALF * PACK], BF16, "hin%d_%d" % (half, b))
-               for half in range(2) for b in range(NB)}
-        hw = {(half, b): held([P, HALF], U32, "hw%d_%d" % (half, b))
-              for half in range(2) for b in range(NB)}
-        hs = {(half, b): held([P, HALF], U8, "hs%d_%d" % (half, b))
-              for half in range(2) for b in range(NB)}
+        hin = [held([P, NB, HALF * PACK], BF16, "hin%d" % half) for half in range(2)]
+        hs = [held([P, NB, HALF], U8, "hs%d" % half) for half in range(2)]
+        hw = {}
+
+        banks = [[psum.tile([P, HALF], F32, name="bank%d_%d" % (i, t)) for t in range(PACK)]
+                 for i in range(2)]
+        z_ring = [held([P, PACK, HALF], F32, "z%d" % i) for i in range(3)]
+        rounded = [held([P, PACK * HALF], BF16, "rounded%d" % b) for b in range(NB)]
+        best_ring = [held([P, HALF], F32, "best%d" % i) for i in range(3)]
 
         def load_words(dst, words, a):
             nc.sync.dma_start(out=dst[:].bitcast(I32),
                               in_=words[a].rearrange("p t i -> p (t i)").bitcast(I32))
 
-        def load_plane(dst, scales, a, row0):
+        def load_plane(queue, dst, scales, a, row0):
             for q in range(4):
-                nc.sync.dma_start(
+                queue.dma_start(
                     out=dst[32 * q + row0: 32 * q + row0 + 4, :].bitcast(I32),
                     in_=scales[a, 4 * q: 4 * q + 4, :].bitcast(I32))
 
         dfc = {}
 
         def load_defence(half, b):
-            tag = "w1raw%d" % b if half == 1 else "dfc%d" % b
-            dfc[(half, b)] = keep.tile([P, PACK, HALF], F32, name="dfc", tag=tag, align_bytes=64)
             rows = defence[PASS * b: PASS * (b + 1), HALF * half: HALF * (half + 1)]
-            nc.sync.dma_start(out=dfc[(half, b)][:], in_=rows.rearrange("(p t) n -> p t n", t=PACK))
+            rows = rows.rearrange("(p t) n -> p t n", t=PACK)
+            pairs = [held([P, 2, HALF], F32, "dfc%d_%d_%d" % (half, b, u)) for u in range(2)]
+            for u in range(2):
+                nc.sync.dma_start(out=pairs[u][:], in_=rows[:, 2 * u: 2 * u + 2, :])
+            dfc[(half, b)] = [pairs[t // 2][:, t % 2, :] for t in range(PACK)]
 
         def load_w1(b):
             nc.sync.dma_start(
@@ -97,9 +102,9 @@ def tile_list_keeper_save_scores_kernel(
         def load_wgo(i):
             nc.sync.dma_start(out=wgo_sb[i][:], in_=wgo[:, HALF * i: HALF * (i + 1)])
 
-        def quantize_w1(b):
-            w1b = work.tile([P, PASS * PACK], BF16, name="w1b", align_bytes=64)
-            nc.scalar.copy(
+        def quantize_w1(b, copy):
+            w1b = rounded[b]
+            copy(
                 out=w1b[:].rearrange("p (t g i j) -> p g j i t", t=PACK, i=2, j=PACK),
                 in_=w1raw[b][:].rearrange("p j (g i t) -> p g j i t", i=2, t=PACK))
             nc.vector.quantize_mx(out=w1w[b][:].bitcast(FP8X4), scales=w1s[b][:], in_=w1b[:])
@@ -108,167 +113,165 @@ def tile_list_keeper_save_scores_kernel(
             return idx[:, HALF * half // 16: HALF * (half + 1) // 16]
 
         def gather_v1(half):
-            nc.vector.tensor_copy(vw[1][:, HALF * half: HALF * (half + 1)],
-                                  tabw[1][:].indirect(list_half(idx1, half)))
+            vw1[half] = keep.tile([P, HALF], U32, name="vw1", tag="w1raw1" if half else "vw1", align_bytes=64)
+            nc.vector.tensor_copy(vw1[half][:], tabw[1][:].indirect(list_half(idx1, half)))
 
         zs = {}
 
-        def throw_sums(half, b):
+        def throw_sums(half, b, slots=range(PACK)):
             cols = slice(HALF * half, HALF * (half + 1))
-            z = work.tile([P, PACK, HALF], F32, name="z", bufs=3)
-            for t in range(PACK):
-                y = psum.tile([P, HALF], F32, name="y", bufs=4)
+            z = z_ring[(NB * half + b) % len(z_ring)]
+            for t in slots:
+                y = banks[b][t]
                 wc = slice(P * t, P * (t + 1))
                 r0 = PASS * b + P * t
                 nc.tensor.matmul_mx(
                     out=y[:], lhsT=w1w[b][:, wc].bitcast(FP8X4), lhsT_scale=w1s[b][:, wc],
-                    rhs=vw[0][:, cols].bitcast(FP8X4), rhs_scale=vs[V_PLANE[0]:P, cols],
+                    rhs=vw0[:, cols].bitcast(FP8X4), rhs_scale=vs[V_PLANE[0]:P, cols],
                     start=True, stop=False)
                 nc.tensor.matmul_mx(
                     out=y[:], lhsT=w4w[:, 2 * r0: 2 * (r0 + P)].bitcast(FP4X4),
                     lhsT_scale=w4s[:, r0: r0 + P],
-                    rhs=vw[1][:, cols].bitcast(FP8X4), rhs_scale=vs[V_PLANE[1]:P, cols],
+                    rhs=vw1[half][:].bitcast(FP8X4), rhs_scale=vs[V_PLANE[1]:P, cols],
                     start=False, stop=True)
-                nc.vector.tensor_tensor(z[:, t, :], y[:], dfc[(half, b)][:, t, :], ALU.add)
+                nc.vector.tensor_tensor(z[:, t, :], y[:], dfc[(half, b)][t], ALU.add)
             zs[(half, b)] = z
 
         def make_h(half, b):
             z = zs[(half, b)]
-            if (half, b) == (0, 0):
-                th = held([P, PACK * HALF], F32, "th")
-                nc.scalar.activation(
-                    out=th[:].rearrange("p (g i t) -> p g t i", i=4, t=PACK),
-                    in_=z[:].rearrange("p t (g i) -> p g t i", i=4), func=ACT.Tanh)
-                nc.vector.tensor_tensor(
-                    hin[(half, b)][:].rearrange("p (n t) -> p n t", t=PACK),
-                    th[:].rearrange("p (n t) -> p n t", t=PACK),
-                    gain_sb[:, b, :].rearrange("p (o t) -> p o t", o=1).to_broadcast([P, HALF, PACK]),
-                    ALU.mult)
-            else:
-                flat = z[:].rearrange("p t n -> p (t n)")
-                nc.scalar.activation(out=flat, in_=flat, func=ACT.Tanh)
-                hb = work.tile([P, PACK, HALF], BF16, name="hb", tag="w1b", align_bytes=64)
-                for t in range(PACK):
-                    nc.scalar.activation(out=hb[:, t, :], in_=z[:, t, :],
-                                         func=ACT.Copy, scale=gain_sb[:, b, t: t + 1])
-                nc.scalar.copy(
-                    out=hin[(half, b)][:].rearrange("p (g i t) -> p g t i", i=8, t=PACK),
-                    in_=hb[:].rearrange("p t (g i) -> p g t i", i=8))
+            hb = rounded[b][:].rearrange("p (t n) -> p t n", t=PACK)
+            for t0 in range(0, PACK, 2):
+                pair = z[:, t0: t0 + 2, :].rearrange("p t n -> p (t n)")
+                nc.scalar.activation(out=pair, in_=pair, func=ACT.Tanh)
+            for t in range(PACK):
+                nc.scalar.activation(out=hb[:, t, :], in_=z[:, t, :],
+                                     func=ACT.Copy, scale=gain_sb[:, b, t: t + 1])
+            nc.scalar.copy(
+                out=hin[half][:, b, :].rearrange("p (g i t) -> p g t i", i=8, t=PACK),
+                in_=hb.rearrange("p t (g i) -> p g t i", i=8))
 
-        def quantize_h(half, b):
-            nc.vector.quantize_mx(out=hw[(half, b)][:].bitcast(FP8X4), scales=hs[(half, b)][:],
-                                  in_=hin[(half, b)][:])
+        def quantize_h(half, blocks, tag):
+            codes = keep.tile([P, len(blocks), HALF], U32, name="hw", tag=tag, align_bytes=64)
+            bs = slice(blocks[0], blocks[-1] + 1)
+            nc.vector.quantize_mx(out=codes[:].rearrange("p b n -> p (b n)").bitcast(FP8X4),
+                                  scales=hs[half][:, bs, :].rearrange("p b n -> p (b n)"),
+                                  in_=hin[half][:, bs, :].rearrange("p b n -> p (b n)"))
+            for i, b in enumerate(blocks):
+                hw[(half, b)] = codes[:, i, :]
 
-        def profile_sum(name, m, words, scales):
+        def profile_sum(acc, m, words, scales):
             mc = slice(P * m, P * (m + 1))
-            acc = psum.tile([P, HALF], F32, name=name)
-            for a in range(2):
+            for a in (1, 0):
                 nc.tensor.matmul_mx(
                     out=acc[:], lhsT=v2w[a][:, mc].bitcast(FP8X4), lhsT_scale=v2s[V2_PLANE[a]:P, mc],
-                    rhs=words[a].bitcast(FP8X4), rhs_scale=scales[a], start=(a == 0), stop=(a == 1))
+                    rhs=words[a].bitcast(FP8X4), rhs_scale=scales[a], start=(a == 1), stop=(a == 0))
             return acc
 
         direct = {}
 
         def direct_scores(half, m):
             cols = slice(HALF * half, HALF * (half + 1))
-            d = profile_sum("d", m, [vw[a][:, cols] for a in range(2)],
+            d = profile_sum(banks[half][m], m, [vw0[:, cols], vw1[half][:]],
                             [vs[V_PLANE[a]:P, cols] for a in range(2)])
-            dsb = work.tile([P, HALF], F32, name="dsb", bufs=2)
-            nc.scalar.copy(out=dsb[:], in_=d[:])
+            dsb = zs[(half, 1)][:, m, :]
+            nc.scalar.copy(out=dsb, in_=d[:])
             direct[(half, m)] = dsb
 
         best = {}
 
         def best_scores(half, m):
-            e = profile_sum("e", m, [hw[(half, b)][:] for b in range(NB)],
-                            [hs[(half, b)][:] for b in range(NB)])
-            bst = work.tile([P, HALF], F32, name="bst", bufs=3)
-            nc.vector.scalar_tensor_tensor(bst[:], e[:], keeper_sb[:, m: m + 1],
-                                           direct[(half, m)][:], ALU.mult, ALU.max)
+            e = profile_sum(banks[1 - half][m], m, [hw[(half, b)] for b in range(NB)],
+                            [hs[half][:, b, :] for b in range(NB)])
+            if (half, m) == (0, 3):
+                bst = hin[1][:, 0, :].bitcast(F32)[:, 0:HALF]
+            elif (half, m) == (0, 2):
+                bst = held([P, HALF], F32, "best_own")[:]
+            else:
+                bst = best_ring[m % len(best_ring)][:]
+            nc.vector.scalar_tensor_tensor(bst, e[:], keeper_sb[:, m: m + 1],
+                                           direct[(half, m)], ALU.mult, ALU.max)
             best[(half, m)] = bst
 
         def place(half, m):
             nc.vector.tensor_tensor(page[m][:].indirect(list_half(idx3, half)),
-                                    best[(half, m)][:], wgo_sb[half][:], ALU.mult)
+                                    best[(half, m)], wgo_sb[half][:], ALU.mult)
             if half == 1:
                 nc.sync.dma_start(out=out[P * m: P * (m + 1), :], in_=page[m][:])
 
         nc.vector.memset(tabs[:].bitcast(I32), 0)
         nc.gpsimd.memset(w4sraw[:].bitcast(I32), 0)
+        load_plane(nc.gpsimd, w4sraw, w4_scales, 0, 0)
         nc.gpsimd.memset(tab2s[:].bitcast(I32), 0)
         nc.sync.dma_start(idx1[:], offs)
         nc.sync.dma_start(out=w4raw[:].bitcast(I32), in_=w4_words[0].bitcast(I32))
-        load_plane(tabs, tab_scales, 0, V_PLANE[0])
+        load_plane(nc.sync, tabs, tab_scales, 0, V_PLANE[0])
         load_words(tabw[0], tab_words, 0)
         load_w1(0)
-        load_plane(tabs, tab_scales, 1, V_PLANE[1])
+        load_plane(nc.sync, tabs, tab_scales, 1, V_PLANE[1])
         nc.sync.dma_start(idx2[:], offs2)
         nc.sync.dma_start(out=gain_sb[:], in_=gain.rearrange("(b p t) -> p b t", b=NB, t=PACK))
         load_words(tabw[1], tab_words, 1)
-        load_plane(w4sraw, w4_scales, 0, 0)
+        load_defence(0, 0)
         load_w1(1)
+        load_defence(0, 1)
         for q in range(4):
             nc.sync.dma_start(
                 out=tab2s[32 * q + V2_PLANE[0]: 32 * q + V2_PLANE[0] + 8, :].bitcast(I32),
                 in_=tab2_scales[:, 4 * q: 4 * q + 4, :].bitcast(I32))
-
-        nc.vector.tensor_copy(
-            out=w4w[:].bitcast(U16).rearrange("p (b t m) -> p b t m", b=NB, t=PACK),
-            in_=w4raw[:].bitcast(U16).rearrange("p (b m t) -> p b t m", b=NB, t=PACK))
-        nc.vector.tensor_copy(vw[0][:], tabw[0][:].indirect(idx1[:]))
-        nc.vector.tensor_copy(vs[:], tabs[:].indirect(idx1[:]))
-        quantize_w1(0)
-        gather_v1(0)
-        gather_v1(1)
-        nc.vector.tensor_copy(
-            out=w4s[:].rearrange("p (b t m) -> p b t m", b=NB, t=PACK),
-            in_=w4sraw[:].rearrange("p (b m t) -> p b t m", b=NB, t=PACK))
-        quantize_w1(1)
-
-        load_defence(0, 0)
-        load_defence(0, 1)
         load_words(tab2w[0], tab2_words, 0)
         nc.sync.dma_start(out=keeper_sb[:], in_=keeper.rearrange("(m p) -> p m", p=P),
                           allow_slow_non_contiguous=True)
         nc.sync.dma_start(idx3[:], offs3)
         load_words(tab2w[1], tab2_words, 1)
+
+        nc.vector.tensor_copy(
+            out=w4w[:].bitcast(U16).rearrange("p (b t m) -> p b t m", b=NB, t=PACK),
+            in_=w4raw[:].bitcast(U16).rearrange("p (b m t) -> p b t m", b=NB, t=PACK))
+        for b in range(NB):
+            rs = slice(PASS * b, PASS * (b + 1))
+            nc.gpsimd.tensor_copy(out=w4s[:, rs].rearrange("p (t m) -> p t m", t=PACK),
+                                  in_=w4sraw[:, rs].rearrange("p (m t) -> p t m", t=PACK))
+        nc.vector.tensor_copy(vw0[:], tabw[0][:].indirect(idx1[:]))
+        nc.vector.tensor_copy(vs[:], tabs[:].indirect(idx1[:]))
+        quantize_w1(0, nc.scalar.copy)
+        gather_v1(0)
+        throw_sums(0, 0)
+        make_h(0, 0)
+        quantize_w1(1, nc.vector.tensor_copy)
+        gather_v1(1)
+        nc.vector.tensor_copy(v2s[:], tab2s[:].indirect(idx2[:]))
+
         load_defence(1, 0)
+        load_defence(1, 1)
         load_wgo(0)
         load_page(0)
-        load_defence(1, 1)
         load_page(1)
         load_page(2)
         load_wgo(1)
         load_page(3)
 
-        nc.vector.tensor_copy(v2s[:], tab2s[:].indirect(idx2[:]))
-        throw_sums(0, 0)
         throw_sums(0, 1)
-        make_h(0, 0)
         make_h(0, 1)
         for a in range(2):
             nc.vector.tensor_copy(v2w[a][:], tab2w[a][:].indirect(idx2[:]))
-        quantize_h(0, 0)
+        quantize_h(0, [0], "dfc0_1_1")
         throw_sums(1, 0)
-        quantize_h(0, 1)
+        throw_sums(1, 1, (0, 1))
+        quantize_h(0, [1], "dfc1_1_0")
+        throw_sums(1, 1, (2, 3))
         for m in range(NM):
             direct_scores(0, m)
+        for m in range(NM - 1):
+            best_scores(0, m)
+        for m in range(NM - 1):
+            place(0, m)
         make_h(1, 0)
-        best_scores(0, 0)
-        best_scores(0, 1)
-        place(0, 0)
-        throw_sums(1, 1)
         make_h(1, 1)
-        best_scores(0, 2)
-        place(0, 1)
-        best_scores(0, 3)
-        place(0, 2)
-        quantize_h(1, 0)
-        place(0, 3)
+        quantize_h(1, [0, 1], "best_own")
+        best_scores(0, NM - 1)
+        place(0, NM - 1)
         for m in range(NM):
             direct_scores(1, m)
-        quantize_h(1, 1)
         best_scores(1, 0)
         for m in range(NM):
             if m + 1 < NM:

@@ -161,10 +161,10 @@ def tile_list_keeper_save_scores_kernel(
 
         def profile_sum(acc, m, words, scales):
             mc = slice(P * m, P * (m + 1))
-            for a in (1, 0):
+            for a in range(2):
                 nc.tensor.matmul_mx(
                     out=acc[:], lhsT=v2w[a][:, mc].bitcast(FP8X4), lhsT_scale=v2s[V2_PLANE[a]:P, mc],
-                    rhs=words[a].bitcast(FP8X4), rhs_scale=scales[a], start=(a == 1), stop=(a == 0))
+                    rhs=words[a].bitcast(FP8X4), rhs_scale=scales[a], start=(a == 0), stop=(a == 1))
             return acc
 
         direct = {}
@@ -182,19 +182,17 @@ def tile_list_keeper_save_scores_kernel(
         def best_scores(half, m):
             e = profile_sum(banks[1 - half][m], m, [hw[(half, b)] for b in range(NB)],
                             [hs[half][:, b, :] for b in range(NB)])
-            if (half, m) == (0, 3):
-                bst = hin[1][:, 0, :].bitcast(F32)[:, 0:HALF]
-            elif (half, m) == (0, 2):
-                bst = held([P, HALF], F32, "best_own")[:]
+            if (half, m) == (0, 2):
+                bst = held([P, HALF], F32, "best_own")
             else:
-                bst = best_ring[m % len(best_ring)][:]
-            nc.vector.scalar_tensor_tensor(bst, e[:], keeper_sb[:, m: m + 1],
+                bst = best_ring[(NM * half + m) % len(best_ring)]
+            nc.vector.scalar_tensor_tensor(bst[:], e[:], keeper_sb[:, m: m + 1],
                                            direct[(half, m)], ALU.mult, ALU.max)
             best[(half, m)] = bst
 
         def place(half, m):
             nc.vector.tensor_tensor(page[m][:].indirect(list_half(idx3, half)),
-                                    best[(half, m)], wgo_sb[half][:], ALU.mult)
+                                    best[(half, m)][:], wgo_sb[half][:], ALU.mult)
             if half == 1:
                 nc.sync.dma_start(out=out[P * m: P * (m + 1), :], in_=page[m][:])
 
@@ -259,21 +257,15 @@ def tile_list_keeper_save_scores_kernel(
         throw_sums(1, 1, (0, 1))
         quantize_h(0, [1], "dfc1_1_0")
         throw_sums(1, 1, (2, 3))
-        for m in range(NM):
-            direct_scores(0, m)
-        for m in range(NM - 1):
-            best_scores(0, m)
-        for m in range(NM - 1):
-            place(0, m)
-        make_h(1, 0)
-        make_h(1, 1)
-        quantize_h(1, [0, 1], "best_own")
-        best_scores(0, NM - 1)
-        place(0, NM - 1)
-        for m in range(NM):
-            direct_scores(1, m)
-        best_scores(1, 0)
-        for m in range(NM):
-            if m + 1 < NM:
-                best_scores(1, m + 1)
-            place(1, m)
+        for half in range(2):
+            for m in range(NM):
+                direct_scores(half, m)
+            best_scores(half, 0)
+            for m in range(NM):
+                if m + 1 < NM:
+                    best_scores(half, m + 1)
+                place(half, m)
+            if half == 0:
+                for b, tag in enumerate(("best_own", "wgo0")):
+                    make_h(1, b)
+                    quantize_h(1, [b], tag)

@@ -69,7 +69,7 @@ def tile_list_keeper_save_scores_kernel(
                  for i in range(2)]
         z_ring = [held([P, PACK, HALF], F32, "z%d" % i) for i in range(3)]
         rounded = [held([P, PACK * HALF], BF16, "rounded%d" % b) for b in range(NB)]
-        best_ring = [held([P, HALF], F32, "best%d" % i) for i in range(3)]
+        best_ring = [held([P, HALF], F32, "best%d" % i) for i in range(4)]
 
         def load_words(dst, words, a):
             nc.sync.dma_start(out=dst[:].bitcast(I32),
@@ -200,6 +200,11 @@ def tile_list_keeper_save_scores_kernel(
         nc.gpsimd.memset(w4sraw[:].bitcast(I32), 0)
         load_plane(nc.gpsimd, w4sraw, w4_scales, 0, 0)
         nc.gpsimd.memset(tab2s[:].bitcast(I32), 0)
+        for q in range(4):
+            nc.gpsimd.dma_start(
+                out=tab2s[32 * q + V2_PLANE[0]: 32 * q + V2_PLANE[0] + 8, :].bitcast(I32),
+                in_=tab2_scales[:, 4 * q: 4 * q + 4, :].bitcast(I32))
+        nc.gpsimd.dma_start(out=gain_sb[:], in_=gain.rearrange("(b p t) -> p b t", b=NB, t=PACK))
         nc.sync.dma_start(idx1[:], offs)
         nc.sync.dma_start(out=w4raw[:].bitcast(I32), in_=w4_words[0].bitcast(I32))
         load_plane(nc.sync, tabs, tab_scales, 0, V_PLANE[0])
@@ -207,19 +212,11 @@ def tile_list_keeper_save_scores_kernel(
         load_w1(0)
         load_plane(nc.sync, tabs, tab_scales, 1, V_PLANE[1])
         nc.sync.dma_start(idx2[:], offs2)
-        nc.sync.dma_start(out=gain_sb[:], in_=gain.rearrange("(b p t) -> p b t", b=NB, t=PACK))
         load_words(tabw[1], tab_words, 1)
         load_defence(0, 0)
         load_w1(1)
         load_defence(0, 1)
-        for q in range(4):
-            nc.sync.dma_start(
-                out=tab2s[32 * q + V2_PLANE[0]: 32 * q + V2_PLANE[0] + 8, :].bitcast(I32),
-                in_=tab2_scales[:, 4 * q: 4 * q + 4, :].bitcast(I32))
         load_words(tab2w[0], tab2_words, 0)
-        nc.sync.dma_start(out=keeper_sb[:], in_=keeper.rearrange("(m p) -> p m", p=P),
-                          allow_slow_non_contiguous=True)
-        nc.sync.dma_start(idx3[:], offs3)
         load_words(tab2w[1], tab2_words, 1)
 
         nc.vector.tensor_copy(
@@ -232,15 +229,18 @@ def tile_list_keeper_save_scores_kernel(
         nc.vector.tensor_copy(vw0[:], tabw[0][:].indirect(idx1[:]))
         nc.vector.tensor_copy(vs[:], tabs[:].indirect(idx1[:]))
         quantize_w1(0, nc.scalar.copy)
+        nc.vector.tensor_copy(v2s[:], tab2s[:].indirect(idx2[:]))
         gather_v1(0)
         throw_sums(0, 0)
         make_h(0, 0)
         quantize_w1(1, nc.vector.tensor_copy)
         gather_v1(1)
-        nc.vector.tensor_copy(v2s[:], tab2s[:].indirect(idx2[:]))
 
         load_defence(1, 0)
         load_defence(1, 1)
+        nc.sync.dma_start(out=keeper_sb[:], in_=keeper.rearrange("(m p) -> p m", p=P),
+                          allow_slow_non_contiguous=True)
+        nc.sync.dma_start(idx3[:], offs3)
         load_wgo(0)
         load_page(0)
         load_page(1)

from contextlib import ExitStack

import concourse.mybir as mybir

F32 = mybir.dt.float32
BF16 = mybir.dt.bfloat16
I32 = mybir.dt.int32
U32 = mybir.dt.uint32
U16 = mybir.dt.uint16
U8 = mybir.dt.uint8
FP8X4 = mybir.dt.float8_e4m3fn_x4
FP4X4 = mybir.dt.float4_e2m1fn_x4
ACT = mybir.ActivationFunctionType
ALU = mybir.AluOpType

P = 128
K, K1, H, T, S, T3, S2, T2 = 1024, 512, 1024, 4096, 1024, 2048, 512, 2048
PACK = 4
PASS = P * PACK
HALF = S // 2
NB = H // PASS
NM = S2 // P
V_PLANE = (4, 0)
V2_PLANE = (8, 12)

FLOPS = 2 * K * H * S + 2 * 2 * H * S2 * S


def tile_list_keeper_save_scores_kernel(
    tc, tab_words, tab_scales, offs, tab2_words, tab2_scales, offs2, offs3,
    w1, w4_words, w4_scales, defence, gain, keeper, page1, wgo, out,
):
    nc = tc.nc
    with ExitStack() as ctx:
        keep = ctx.enter_context(tc.tile_pool(name="keep", bufs=1))
        psum = ctx.enter_context(tc.psum_pool(name="psum", bufs=1))

        def held(shape, dtype, name):
            return keep.tile(shape, dtype, name=name, align_bytes=64)

        idx1 = held([P, S // 16], U16, "idx1")
        idx2 = held([P, S2 // 16], U16, "idx2")
        idx3 = held([P, S // 16], U16, "idx3")
        tabw = [held([P, T], U32, "tabw%d" % a) for a in range(2)]
        tabs = held([P, T], U8, "tabs")
        tab2w = [held([P, T3], U32, "tab2w%d" % a) for a in range(2)]
        tab2s = held([P, T3], U8, "tab2s")
        w1raw = [held([P, PACK, PASS], F32, "w1raw%d" % b) for b in range(NB)]
        w4raw = held([P, 2 * H], U8, "w4raw")
        w4sraw = held([P, H], U8, "w4sraw")
        w4w = held([P, 2 * H], U8, "w4w")
        w4s = held([P, H], U8, "w4s")
        w1w = [held([P, PASS], U32, "w1w%d" % b) for b in range(NB)]
        w1s = [held([P, PASS], U8, "w1s%d" % b) for b in range(NB)]
        gain_sb = held([P, NB, PACK], F32, "gain_sb")
        keeper_sb = held([P, NM], F32, "keeper_sb")
        wgo_sb = [held([P, HALF], F32, "wgo%d" % i) for i in range(2)]
        page = [held([P, T2], F32, "page%d" % m) for m in range(NM)]
        vw0 = held([P, S], U32, "vw0")
        vw1 = {}
        vs = held([P, S], U8, "vs")
        v2w = [held([P, S2], U32, "v2w%d" % a) for a in range(2)]
        v2s = held([P, S2], U8, "v2s")
        hin = [held([P, NB, HALF * PACK], BF16, "hin%d" % half) for half in range(2)]
        hs = [held([P, NB, HALF], U8, "hs%d" % half) for half in range(2)]
        hw = {}

        banks = [[psum.tile([P, HALF], F32, name="bank%d_%d" % (i, t)) for t in range(PACK)]
                 for i in range(2)]
        z_ring = [held([P, PACK, HALF], F32, "z%d" % i) for i in range(3)]
        rounded = [held([P, PACK * HALF], BF16, "rounded%d" % b) for b in range(NB)]
        best_ring = [held([P, HALF], F32, "best%d" % i) for i in range(4)]

        def load_words(dst, words, a):
            nc.sync.dma_start(out=dst[:].bitcast(I32),
                              in_=words[a].rearrange("p t i -> p (t i)").bitcast(I32))

        def load_plane(queue, dst, scales, a, row0):
            for q in range(4):
                queue.dma_start(
                    out=dst[32 * q + row0: 32 * q + row0 + 4, :].bitcast(I32),
                    in_=scales[a, 4 * q: 4 * q + 4, :].bitcast(I32))

        dfc = {}

        def load_defence(half, b):
            rows = defence[PASS * b: PASS * (b + 1), HALF * half: HALF * (half + 1)]
            rows = rows.rearrange("(p t) n -> p t n", t=PACK)
            pairs = [held([P, 2, HALF], F32, "dfc%d_%d_%d" % (half, b, u)) for u in range(2)]
            for u in range(2):
                nc.sync.dma_start(out=pairs[u][:], in_=rows[:, 2 * u: 2 * u + 2, :])
            dfc[(half, b)] = [pairs[t // 2][:, t % 2, :] for t in range(PACK)]

        def load_w1(b):
            nc.sync.dma_start(
                out=w1raw[b][:],
                in_=w1[:, PASS * b: PASS * (b + 1)].rearrange("(p j) r -> p j r", j=PACK))

        def load_page(m):
            nc.sync.dma_start(out=page[m][:], in_=page1[P * m: P * (m + 1), :])

        def load_wgo(i):
            nc.sync.dma_start(out=wgo_sb[i][:], in_=wgo[:, HALF * i: HALF * (i + 1)])

        def quantize_w1(b, copy):
            w1b = rounded[b]
            copy(
                out=w1b[:].rearrange("p (t g i j) -> p g j i t", t=PACK, i=2, j=PACK),
                in_=w1raw[b][:].rearrange("p j (g i t) -> p g j i t", i=2, t=PACK))
            nc.vector.quantize_mx(out=w1w[b][:].bitcast(FP8X4), scales=w1s[b][:], in_=w1b[:])

        def list_half(idx, half):
            return idx[:, HALF * half // 16: HALF * (half + 1) // 16]

        def gather_v1(half):
            vw1[half] = keep.tile([P, HALF], U32, name="vw1", tag="w1raw1" if half else "vw1", align_bytes=64)
            nc.vector.tensor_copy(vw1[half][:], tabw[1][:].indirect(list_half(idx1, half)))

        zs = {}

        def throw_sums(half, b, slots=range(PACK)):
            cols = slice(HALF * half, HALF * (half + 1))
            z = z_ring[(NB * half + b) % len(z_ring)]
            for t in slots:
                y = banks[b][t]
                wc = slice(P * t, P * (t + 1))
                r0 = PASS * b + P * t
                nc.tensor.matmul_mx(
                    out=y[:], lhsT=w1w[b][:, wc].bitcast(FP8X4), lhsT_scale=w1s[b][:, wc],
                    rhs=vw0[:, cols].bitcast(FP8X4), rhs_scale=vs[V_PLANE[0]:P, cols],
                    start=True, stop=False)
                nc.tensor.matmul_mx(
                    out=y[:], lhsT=w4w[:, 2 * r0: 2 * (r0 + P)].bitcast(FP4X4),
                    lhsT_scale=w4s[:, r0: r0 + P],
                    rhs=vw1[half][:].bitcast(FP8X4), rhs_scale=vs[V_PLANE[1]:P, cols],
                    start=False, stop=True)
                nc.vector.tensor_tensor(z[:, t, :], y[:], dfc[(half, b)][t], ALU.add)
            zs[(half, b)] = z

        def make_h(half, b):
            z = zs[(half, b)]
            hb = rounded[b][:].rearrange("p (t n) -> p t n", t=PACK)
            for t0 in range(0, PACK, 2):
                pair = z[:, t0: t0 + 2, :].rearrange("p t n -> p (t n)")
                nc.scalar.activation(out=pair, in_=pair, func=ACT.Tanh)
            for t in range(PACK):
                nc.scalar.activation(out=hb[:, t, :], in_=z[:, t, :],
                                     func=ACT.Copy, scale=gain_sb[:, b, t: t + 1])
            nc.scalar.copy(
                out=hin[half][:, b, :].rearrange("p (g i t) -> p g t i", i=8, t=PACK),
                in_=hb.rearrange("p t (g i) -> p g t i", i=8))

        def quantize_h(half, blocks, tag):
            codes = keep.tile([P, len(blocks), HALF], U32, name="hw", tag=tag, align_bytes=64)
            bs = slice(blocks[0], blocks[-1] + 1)
            nc.vector.quantize_mx(out=codes[:].rearrange("p b n -> p (b n)").bitcast(FP8X4),
                                  scales=hs[half][:, bs, :].rearrange("p b n -> p (b n)"),
                                  in_=hin[half][:, bs, :].rearrange("p b n -> p (b n)"))
            for i, b in enumerate(blocks):
                hw[(half, b)] = codes[:, i, :]

        def profile_sum(acc, m, words, scales):
            mc = slice(P * m, P * (m + 1))
            for a in range(2):
                nc.tensor.matmul_mx(
                    out=acc[:], lhsT=v2w[a][:, mc].bitcast(FP8X4), lhsT_scale=v2s[V2_PLANE[a]:P, mc],
                    rhs=words[a].bitcast(FP8X4), rhs_scale=scales[a], start=(a == 0), stop=(a == 1))
            return acc

        direct = {}

        def direct_scores(half, m):
            cols = slice(HALF * half, HALF * (half + 1))
            d = profile_sum(banks[half][m], m, [vw0[:, cols], vw1[half][:]],
                            [vs[V_PLANE[a]:P, cols] for a in range(2)])
            dsb = zs[(half, 1)][:, m, :]
            nc.scalar.copy(out=dsb, in_=d[:])
            direct[(half, m)] = dsb

        best = {}

        def best_scores(half, m):
            e = profile_sum(banks[1 - half][m], m, [hw[(half, b)] for b in range(NB)],
                            [hs[half][:, b, :] for b in range(NB)])
            if (half, m) == (0, 2):
                bst = held([P, HALF], F32, "best_own")
            else:
                bst = best_ring[(NM * half + m) % len(best_ring)]
            nc.vector.scalar_tensor_tensor(bst[:], e[:], keeper_sb[:, m: m + 1],
                                           direct[(half, m)], ALU.mult, ALU.max)
            best[(half, m)] = bst

        def place(half, m):
            nc.vector.tensor_tensor(page[m][:].indirect(list_half(idx3, half)),
                                    best[(half, m)][:], wgo_sb[half][:], ALU.mult)
            if half == 1:
                nc.sync.dma_start(out=out[P * m: P * (m + 1), :], in_=page[m][:])

        nc.vector.memset(tabs[:].bitcast(I32), 0)
        nc.gpsimd.memset(w4sraw[:].bitcast(I32), 0)
        load_plane(nc.gpsimd, w4sraw, w4_scales, 0, 0)
        nc.gpsimd.memset(tab2s[:].bitcast(I32), 0)
        for q in range(4):
            nc.gpsimd.dma_start(
                out=tab2s[32 * q + V2_PLANE[0]: 32 * q + V2_PLANE[0] + 8, :].bitcast(I32),
                in_=tab2_scales[:, 4 * q: 4 * q + 4, :].bitcast(I32))
        nc.gpsimd.dma_start(out=gain_sb[:], in_=gain.rearrange("(b p t) -> p b t", b=NB, t=PACK))
        nc.sync.dma_start(idx1[:], offs)
        nc.sync.dma_start(out=w4raw[:].bitcast(I32), in_=w4_words[0].bitcast(I32))
        load_plane(nc.sync, tabs, tab_scales, 0, V_PLANE[0])
        load_words(tabw[0], tab_words, 0)
        load_w1(0)
        load_plane(nc.sync, tabs, tab_scales, 1, V_PLANE[1])
        nc.sync.dma_start(idx2[:], offs2)
        load_words(tabw[1], tab_words, 1)
        load_defence(0, 0)
        load_w1(1)
        load_defence(0, 1)
        load_words(tab2w[0], tab2_words, 0)
        load_words(tab2w[1], tab2_words, 1)

        nc.vector.tensor_copy(
            out=w4w[:].bitcast(U16).rearrange("p (b t m) -> p b t m", b=NB, t=PACK),
            in_=w4raw[:].bitcast(U16).rearrange("p (b m t) -> p b t m", b=NB, t=PACK))
        for b in range(NB):
            rs = slice(PASS * b, PASS * (b + 1))
            nc.gpsimd.tensor_copy(out=w4s[:, rs].rearrange("p (t m) -> p t m", t=PACK),
                                  in_=w4sraw[:, rs].rearrange("p (m t) -> p t m", t=PACK))
        nc.vector.tensor_copy(vw0[:], tabw[0][:].indirect(idx1[:]))
        nc.vector.tensor_copy(vs[:], tabs[:].indirect(idx1[:]))
        quantize_w1(0, nc.scalar.copy)
        nc.vector.tensor_copy(v2s[:], tab2s[:].indirect(idx2[:]))
        gather_v1(0)
        throw_sums(0, 0)
        make_h(0, 0)
        quantize_w1(1, nc.vector.tensor_copy)
        gather_v1(1)

        load_defence(1, 0)
        load_defence(1, 1)
        nc.sync.dma_start(out=keeper_sb[:], in_=keeper.rearrange("(m p) -> p m", p=P),
                          allow_slow_non_contiguous=True)
        nc.sync.dma_start(idx3[:], offs3)
        load_wgo(0)
        load_page(0)
        load_page(1)
        load_page(2)
        load_wgo(1)
        load_page(3)

        throw_sums(0, 1)
        make_h(0, 1)
        for a in range(2):
            nc.vector.tensor_copy(v2w[a][:], tab2w[a][:].indirect(idx2[:]))
        quantize_h(0, [0], "dfc0_1_1")
        throw_sums(1, 0)
        throw_sums(1, 1, (0, 1))
        quantize_h(0, [1], "dfc1_1_0")
        throw_sums(1, 1, (2, 3))
        for half in range(2):
            for m in range(NM):
                direct_scores(half, m)
            best_scores(half, 0)
            for m in range(NM):
                if m + 1 < NM:
                    best_scores(half, m + 1)
                place(half, m)
            if half == 0:
                for b, tag in enumerate(("best_own", "wgo0")):
                    make_h(1, b)
                    quantize_h(1, [b], tag)
